import numpy as np
import ml_dtypes


def mxq(x, axis, fmt="e4m3"):
    dtype, down = {"e4m3": (ml_dtypes.float8_e4m3fn, 7), "e5m2": (ml_dtypes.float8_e5m2, 14)}[fmt]
    v = np.moveaxis(np.asarray(x, np.float32).astype(ml_dtypes.bfloat16).astype(np.float64), axis, -1)
    blocks = v.reshape(v.shape[:-1] + (-1, 32))
    amax = np.abs(blocks).max(-1, keepdims=True)
    byte = np.maximum(np.where(amax > 0, np.frexp(amax)[1] - 1 + 127, 0) - down, 1)
    scale = np.exp2(byte - 127.0)
    codes = (blocks / scale).astype(np.float32).astype(dtype).astype(np.float64)
    return np.moveaxis((codes * scale).reshape(v.shape), -1, axis)


WIDE = False


def mx_kscale(k):
    if not WIDE:
        return np.ones(k)
    levels = np.array([10, -10, 5, -5, 0])
    if k % 512:
        return np.exp2(np.random.permutation(np.resize(levels, k // 32))).repeat(32)
    a = np.empty((k // 512, 16))
    for p in range(k // 512):
        a[p, :8] = np.random.permutation(np.resize(levels, 8))
        for g in range(8):
            far = levels[np.abs(levels - a[p, g]) >= 10]
            a[p, g + 8] = far[np.random.randint(len(far))]
    return np.exp2(a.ravel()).repeat(32)


def f64(x):
    return np.asarray(x).astype(np.float64)


def striped(idx):
    return np.tile(np.asarray(idx).reshape(-1, 16).T, (8, 1)).astype(np.uint16)


def unstriped(offs):
    return offs[:16].T.reshape(-1).astype(np.int64)


E2M1 = np.array([0.0, 0.5, 1.0, 1.5, 2.0, 3.0, 4.0, 6.0, -0.0, -0.5, -1.0, -1.5, -2.0, -3.0, -4.0, -6.0])


def pack_weight(w, fmt):
    k, n = w.shape
    w = f64(np.asarray(w, np.float32).astype(ml_dtypes.bfloat16)).reshape(k // 32, 32, n)
    amax = np.abs(w).max(1)
    if fmt == "e4m3":
        byte = np.frexp(amax)[1] - 1 + 127 - 7
    else:
        mant, ex = np.frexp(amax / 6.0)
        byte = np.where(mant > 0.5, ex, ex - 1) + 127
    byte = np.clip(np.where(amax > 0, byte, 1), 1, 254)
    scaled = (w * np.exp2(127.0 - byte)[:, None, :]).reshape(k, n).astype(np.float32)
    by_word = np.ascontiguousarray(scaled.reshape(k // 512, 128, 4, n).transpose(0, 1, 3, 2))
    if fmt == "e4m3":
        words = by_word.astype(ml_dtypes.float8_e4m3fn).view(np.uint8)
    else:
        c = by_word.astype(ml_dtypes.float4_e2m1fn).view(np.uint8) & 0xF
        words = (c[..., 0::2] | (c[..., 1::2] << 4)).reshape(k // 512, 128, 2 * n)
    return np.ascontiguousarray(words), np.ascontiguousarray(byte.astype(np.uint8).reshape(k // 512, 16, n))


def unpack_weight(words, scales, fmt):
    g, _, n = scales.shape
    words = np.ascontiguousarray(words).reshape(g, 128, n, -1)
    if fmt == "e4m3":
        vals = words.view(ml_dtypes.float8_e4m3fn).astype(np.float64)
    else:
        nib = np.empty((g, 128, n, 4), np.uint8)
        nib[..., 0::2] = words & 0xF
        nib[..., 1::2] = words >> 4
        vals = E2M1[nib]
    vals = vals * np.repeat(np.exp2(scales.astype(np.float64) - 127.0), 8, axis=1)[..., None]
    return vals.transpose(0, 1, 3, 2).reshape(g * 512, n)


def bf(x):
    return np.asarray(x, np.float32).astype(ml_dtypes.bfloat16)


def planes(Y):
    r, m = Y.shape
    b = f64(bf(Y)).reshape(r // 32, 32, m)
    amax = np.abs(b).max(1)
    byte = np.clip(np.where(amax > 0, np.frexp(amax)[1] - 1 + 127 - 7, 1), 1, 254)
    codes = (b * np.exp2(127.0 - byte)[:, None, :]).reshape(r, m).astype(np.float32).astype(ml_dtypes.float8_e4m3fn).view(np.uint8)
    words = codes.reshape(r // 512, 128, 4, m).transpose(0, 1, 3, 2)
    return np.ascontiguousarray(words), np.ascontiguousarray(byte.astype(np.uint8).reshape(r // 512, 16, m))


D, T, I, Q, E, U, G, K = 512, 2048, 512, 256, 512, 1024, 64, 32


def setup_inputs():
    n = np.random.standard_normal
    idx = np.random.permutation(T)[:I]
    idx2 = np.random.permutation(U)[:I]
    fd = mx_kscale(D)
    fi = mx_kscale(I)
    ti = np.ones(T)
    ti[idx] = fi
    keysp = pack_weight(n((D, T)) / fd[:, None], "e2m1")
    return {
        "query": (n((D, Q)) * 0.9 / np.sqrt(D) * fd[:, None]).astype(np.float32),
        "keys_words": keysp[0],
        "keys_scales": keysp[1],
        "concepts": (n((D, U)) / fd[:, None]).astype(np.float32),
        "part": np.tile(np.random.uniform(0.2, 1.0, T), (128, 1)).astype(np.float32),
        "lam": (np.random.uniform(0.7, 1.4, (Q, 1))).astype(np.float32),
        "shy": (np.random.uniform(20.0, 60.0, (Q, 1))).astype(np.float32),
        "os": (np.random.uniform(4.0, 16.0, (1, I)) * fi).astype(np.float32),
        "vals": (n((E, T)) / ti).astype(np.float32),
        "hold": (np.random.uniform(0.4, 1.0, (1, Q))).astype(np.float32),
        "offs": striped(idx),
        "offs2": striped(idx2),
    }


def reference(query, keys_words, keys_scales, concepts, part, lam, shy, os, vals, hold, offs, offs2):
    idx = unstriped(offs)
    idx2 = unstriped(offs2)
    keysu = unpack_weight(keys_words, keys_scales, "e2m1")
    queryq = mxq(f64(query), 0, "e4m3")
    keysidxg = keysu[:, idx]
    a = queryq.T @ keysidxg
    conceptsidx2q = mxq(f64(concepts)[:, idx2], 0, "e4m3")
    b = queryq.T @ conceptsidx2q
    s = (a - b * f64(part)[:1][:, idx]) * f64(lam)
    p = np.exp(s - np.max(s, axis=1, keepdims=True))
    r = p / np.sum(p, axis=1, keepdims=True)
    pg = r.reshape(Q, G, I // G).sum(axis=2)
    k0 = np.exp(pg * f64(shy) * (-1.0))
    kr = np.repeat(k0, I // G, axis=1)
    u0 = r * kr
    w = u0 / np.sum(u0, axis=1, keepdims=True)
    wo1 = w * f64(os)
    wt1 = wo1.T
    vt1 = f64(vals)[:, idx].T
    vt1q = mxq(vt1, 0, "e4m3")
    wt1q = mxq(wt1, 0, "e4m3")
    o = vt1q.T @ wt1q
    og = o.reshape(E, K, Q // K).mean(axis=2)
    ogr = np.repeat(og, Q // K, axis=1)
    y = o - ogr * f64(hold)
    words, scales = planes(y)
    return y, words, scales

@@ -1,0 +1,333 @@
+from contextlib import ExitStack
+
+import concourse.mybir as mybir
+from concourse.masks import make_identity
+
+F32 = mybir.dt.float32
+BF16 = mybir.dt.bfloat16
+I32 = mybir.dt.int32
+U32 = mybir.dt.uint32
+U16 = mybir.dt.uint16
+U8 = mybir.dt.uint8
+FP8X4 = mybir.dt.float8_e4m3fn_x4
+FP4X4 = mybir.dt.float4_e2m1fn_x4
+ALU = mybir.AluOpType
+ACT = mybir.ActivationFunctionType
+AX = mybir.AxisListType
+
+P = 128
+PACK = 4
+D, T, I, Q, E, U = 512, 2048, 512, 256, 512, 1024
+RUN = 8
+QT = Q // P
+
+FLOPS = 2 * D * Q * I * 2 + 2 * I * E * Q
+
+
+def tile_attend_withoutconcept_crowdshy_beyondgroupread_pl_kernel(
+    tc, query, keys_words, keys_scales, concepts, part, lam, shy, os_, vals, hold, offs, offs2, out_0, out_1, out_2
+):
+    nc = tc.nc
+    with ExitStack() as ctx:
+        sb = ctx.enter_context(tc.tile_pool(name="sb", bufs=1))
+        ps = ctx.enter_context(tc.psum_pool(name="ps", bufs=1))
+
+        def bank(tag):
+            return ps.tile([P, 512], F32, name=tag, tag=tag)
+
+        ks_win = sb.tile([P, T], U8, name="ks_win", align_bytes=64)
+        nc.gpsimd.memset(ks_win[:].bitcast(I32), 0)
+        part_win = sb.tile([P, T], F32, name="part_win", align_bytes=64)
+        nc.vector.memset(part_win[:, 0 : T // 2], 0.0)
+        ident = sb.tile([P, P], F32, name="ident", align_bytes=64)
+        make_identity(nc, ident[:])
+        nc.gpsimd.memset(part_win[:, T // 2 : T], 0.0)
+
+        lam_col = sb.tile([P, QT], F32, name="lam_col")
+        shy_col = sb.tile([P, QT], F32, name="shy_col")
+        os_col = sb.tile([P, PACK], F32, name="os_col")
+        hold_col = sb.tile([P, QT], F32, name="hold_col")
+
+        conc_rows = concepts.rearrange("(p t) u -> t p u", t=PACK)
+        conc_win = [sb.tile([P, U], F32, name=f"conc_win{t}", tag=f"conc_win{t}", align_bytes=64) for t in range(PACK)]
+        val_rows = vals.rearrange("(p j) c -> j p c", j=PACK)
+        val_win = [sb.tile([P, T], F32, name=f"val_win{j}", tag=f"val_win{j}", align_bytes=64) for j in range(PACK)]
+        idx2 = sb.tile([P, I // 16], U16, name="idx2")
+        idx = sb.tile([P, I // 16], U16, name="idx")
+        q_raw = sb.tile([P, PACK, Q], F32, name="q_raw", tag="q_raw", align_bytes=64)
+        kw_win = sb.tile([P, T], U16, name="kw_win", align_bytes=64)
+
+        def load_scale_rows(queue, g):
+            queue.dma_start(
+                ks_win[32 * g : 32 * g + 4, :].bitcast(I32), keys_scales[0, 4 * g : 4 * g + 4, :].bitcast(I32)
+            )
+
+        nc.sync.dma_start(hold_col[:], hold.rearrange("o (p e) -> p (o e)", e=QT))
+        nc.sync.dma_start(idx2[:], offs2)
+        nc.sync.dma_start(idx[:], offs)
+        nc.sync.dma_start(os_col[:], os_.rearrange("o (p t) -> p (o t)", t=PACK))
+        nc.sync.dma_start(conc_win[0][:], conc_rows[0])
+        nc.sync.dma_start(conc_win[1][:], conc_rows[1])
+        load_scale_rows(nc.sync, 0)
+        load_scale_rows(nc.sync, 1)
+        nc.sync.dma_start(part_win[0:1, :], part[0:1, :])
+        load_scale_rows(nc.sync, 2)
+        load_scale_rows(nc.sync, 3)
+        nc.sync.dma_start(conc_win[2][:], conc_rows[2])
+        nc.sync.dma_start(conc_win[3][:], conc_rows[3])
+        nc.sync.dma_start(q_raw[:], query.rearrange("(p t) q -> p t q", t=PACK))
+        nc.sync.dma_start(kw_win[:].bitcast(I32), keys_words[0].bitcast(I32))
+        nc.sync.dma_start(val_win[0][:], val_rows[0])
+        nc.sync.dma_start(val_win[1][:], val_rows[1])
+        nc.sync.dma_start(val_win[2][:], val_rows[2])
+        nc.sync.dma_start(val_win[3][:], val_rows[3])
+        with nc.allow_non_contiguous_dma(reason="one value a partition"):
+            nc.gpsimd.dma_start(lam_col[:], lam.rearrange("(h p) o -> p (h o)", p=P))
+        with nc.allow_non_contiguous_dma(reason="one value a partition"):
+            nc.gpsimd.dma_start(shy_col[:], shy.rearrange("(h p) o -> p (h o)", p=P))
+
+        hold_8th = sb.tile([P, QT], F32, name="hold_8th")
+        nc.scalar.activation(hold_8th[:], hold_col[:], ACT.Copy, scale=1.0 / RUN)
+        spread = bank("misc2")
+        for t in range(PACK):
+            nc.tensor.transpose(spread[:, t * P : (t + 1) * P], os_col[:, t : t + 1].to_broadcast([P, P]), ident[:])
+        os_b = sb.tile([P, I], F32, name="os_b", align_bytes=64)
+        nc.scalar.copy(os_b[:].rearrange("p (s t) -> p s t", t=PACK), spread[:].rearrange("p (t s) -> p s t", t=PACK))
+        spread = bank("misc3")
+        for e in range(QT):
+            nc.tensor.transpose(spread[:, e * P : (e + 1) * P], hold_8th[:, e : e + 1].to_broadcast([P, P]), ident[:])
+        hold_b = sb.tile([P, Q], F32, name="hold_b", align_bytes=64)
+        nc.scalar.copy(
+            hold_b[:].rearrange("p (s e) -> p s e", e=QT),
+            spread[:, 0:Q].rearrange("p (e s) -> p s e", e=QT),
+        )
+
+        conc_g = sb.tile([P, PACK, I], BF16, name="conc_g", align_bytes=64)
+
+        def gather(engine, out, window, offsets):
+            if engine == "scalar":
+                nc.scalar.activation(out, window.indirect(offsets), ACT.Copy)
+            else:
+                nc.vector.tensor_copy(out, window.indirect(offsets))
+
+        def gather_halves(engines, out, window, offsets):
+            for half, engine in enumerate(engines):
+                n = I // len(engines)
+                gather(engine, out[:, half * n : (half + 1) * n], window, offsets[:, half * n // 16 : (half + 1) * n // 16])
+
+        for t, engines in enumerate([["vector"], ["scalar"], ["scalar"], ["scalar", "vector"]]):
+            gather_halves(engines, conc_g[:, t, :], conc_win[t][:], idx2)
+
+        part_g = sb.tile([P, I], F32, name="part_g", align_bytes=64)
+        nc.vector.tensor_copy(part_g[:], part_win[:].indirect(idx[:]))
+        k_scales = sb.tile([P, I], U8, name="k_scales", align_bytes=64)
+        nc.vector.tensor_copy(k_scales[:], ks_win[:].indirect(idx[:]))
+
+        turn = bank("misc0")
+        for c in range(PACK):
+            nc.tensor.transpose(turn[:, c * P : (c + 1) * P], part_g[:, c * P : (c + 1) * P], ident[:])
+        part_col = sb.tile([P, PACK], F32, name="part_col", tag="conc_win3", align_bytes=64)
+        nc.scalar.copy(part_col[:], turn[:, 0 : I : P])
+        part_spread = bank("misc1")
+        for c in range(PACK):
+            nc.tensor.transpose(part_spread[:, c * P : (c + 1) * P], part_col[:, c : c + 1].to_broadcast([P, P]), ident[:])
+        conc_in = sb.tile([P, I * PACK], BF16, name="conc_in", align_bytes=64)
+        nc.vector.tensor_copy(
+            conc_in[:].rearrange("p (c i t) -> p c t i", i=4, t=PACK),
+            conc_g[:].rearrange("p t (c i) -> p c t i", i=4),
+        )
+        c_codes = sb.tile([P, I], U32, name="c_codes", align_bytes=64)
+        c_scales = sb.tile([P, I], U8, name="c_scales", align_bytes=64)
+        nc.vector.quantize_mx(out=c_codes[:].bitcast(FP8X4), scales=c_scales[:], in_=conc_in[:])
+
+        q_in = sb.tile([P, Q * PACK], BF16, name="q_in", tag="q_in", align_bytes=64)
+        nc.scalar.copy(
+            q_in[:].rearrange("p (c i t) -> p c t i", i=4, t=PACK),
+            q_raw[:].rearrange("p t (c i) -> p c t i", i=4),
+        )
+        part_b = sb.tile([P, I], F32, name="part_b", tag="q_raw", align_bytes=64)
+        nc.scalar.copy(part_b[:], part_spread[:])
+
+        q_codes = sb.tile([P, Q], U32, name="q_codes", align_bytes=64)
+        q_scales = sb.tile([P, Q], U8, name="q_scales", align_bytes=64)
+        nc.vector.quantize_mx(out=q_codes[:].bitcast(FP8X4), scales=q_scales[:], in_=q_in[:])
+
+        k_words = sb.tile([P, I], U16, name="k_words", tag="q_in", align_bytes=64)
+        nc.vector.tensor_copy(k_words[:], kw_win[:].indirect(idx[:]))
+
+        a_ps, b_ps = [], []
+        for h in range(QT):
+            cols = slice(h * P, (h + 1) * P)
+            b = bank(f"b{h}")
+            nc.tensor.matmul_mx(
+                out=b[:], lhsT=q_codes[:, cols].bitcast(FP8X4), lhsT_scale=q_scales[:, cols],
+                rhs=c_codes[:].bitcast(FP8X4), rhs_scale=c_scales[:], start=True, stop=True,
+            )
+            b_ps.append(b)
+        for h in range(QT):
+            cols = slice(h * P, (h + 1) * P)
+            a = bank(f"a{h}")
+            nc.tensor.matmul_mx(
+                out=a[:], lhsT=q_codes[:, cols].bitcast(FP8X4), lhsT_scale=q_scales[:, cols],
+                rhs=k_words[:].bitcast(FP4X4), rhs_scale=k_scales[:], start=True, stop=True,
+            )
+            a_ps.append(a)
+
+        v_codes = sb.tile([P, E], U32, name="v_codes", align_bytes=64)
+        v_scales = sb.tile([P, E], U8, name="v_scales", align_bytes=64)
+
+        def values(j):
+            vg = sb.tile([P, I], BF16, name=f"val_g{j}", align_bytes=64)
+            gather_halves(([["scalar", "scalar"]] * 3 + [["scalar"]])[j], vg, val_win[j][:], idx)
+            st["vg", j] = vg
+
+        def turn_values(j, tag):
+            pairs = st["vg", j][:].bitcast(F32)
+            turned = bank(f"misc{j % 2}")
+            for u in range(2):
+                nc.tensor.transpose(turned[:, u * P : (u + 1) * P], pairs[:, u : I // 2 : 2], ident[:])
+            v_in = sb.tile([P, P * PACK], BF16, name=f"v_in{j}", tag=tag, align_bytes=64)
+            nc.scalar.copy(
+                v_in[:].bitcast(F32).rearrange("p (m u) -> p m u", u=2),
+                turned[:, 0 : 2 * P].rearrange("p (u m) -> p m u", u=2),
+            )
+            cols = slice(j * P, (j + 1) * P)
+            nc.vector.quantize_mx(out=v_codes[:, cols].bitcast(FP8X4), scales=v_scales[:, cols], in_=v_in[:])
+
+        w_codes = sb.tile([P, Q], U32, name="w_codes", align_bytes=64)
+        w_scales = sb.tile([P, Q], U8, name="w_scales", align_bytes=64)
+        st = {}
+
+        def small(name, h, n=1):
+            return sb.tile([P, n], F32, name=f"{name}{h}")
+
+        def wide(name, h, tag=None):
+            return sb.tile([P, I], F32, name=f"{name}{h}", tag=tag or f"{name}{h}", align_bytes=64)
+
+        def taken(h):
+            t = wide("taken", h)
+            nc.vector.tensor_tensor(t[:], b_ps[h][:], part_b[:], ALU.mult)
+            st["t", h] = t
+
+        def scores(h):
+            d = wide("diff", h)
+            nc.vector.tensor_tensor(d[:], st["t", h][:], a_ps[h][:], ALU.subtract)
+            ns = wide("negs", h)
+            mn = small("mn", h)
+            nc.vector.tensor_scalar(ns[:], d[:], lam_col[:, h : h + 1], None, ALU.mult, ALU.min, accum_out=mn[:])
+            p = p_all[:, h, :]
+            z = small("z", h)
+            nc.scalar.activation(p, ns[:], ACT.Exp, bias=mn[:], scale=-1.0, accum_out=z[:])
+            st["p", h], st["z", h] = p, z
+
+        def damp(h):
+            p, z = st["p", h], st["z", h]
+            pos = wide("pos", h)
+            nc.gpsimd.tensor_tensor(pos[:], p, os_b[:], ALU.mult)
+            rz = small("rz", h)
+            nc.vector.reciprocal(rz[:], z[:])
+            pg = small("pg", h, I // RUN)
+            nc.vector.tensor_reduce(pg[:], p.rearrange("p (g r) -> p g r", r=RUN), AX.X, ALU.add)
+            c = small("c", h)
+            nc.vector.tensor_scalar(c[:], rz[:], shy_col[:, h : h + 1], -1.0, ALU.mult, ALU.mult)
+            k0 = small("k0", h, I // RUN)
+            nc.scalar.activation(k0[:], pg[:], ACT.Exp, scale=c[:])
+            st["pos", h], st["pg", h], st["k0", h] = pos, pg, k0
+
+        def weights(h):
+            pos, pg, k0 = st["pos", h], st["pg", h], st["k0", h]
+            ug = small("ug", h, I // RUN)
+            den = small("den", h)
+            nc.vector.scalar_tensor_tensor(ug[:], pg[:], 1.0, k0[:], ALU.mult, ALU.mult, accum_out=den[:])
+            rden = small("rden", h)
+            nc.vector.reciprocal(rden[:], den[:])
+            wo = sb.tile([P, I], BF16, name=f"wo{h}", align_bytes=64)
+            nc.vector.scalar_tensor_tensor(
+                wo[:].rearrange("p (g r) -> p g r", r=RUN),
+                pos[:].rearrange("p (g r) -> p g r", r=RUN),
+                rden[:],
+                k0[:].unsqueeze(2).to_broadcast([P, I // RUN, RUN]),
+                ALU.mult, ALU.mult,
+            )
+            pairs = wo[:].bitcast(F32)
+            turned = bank(f"misc{2 + h}")
+            for u in range(2):
+                nc.tensor.transpose(turned[:, u * P : (u + 1) * P], pairs[:, u : I // 2 : 2], ident[:])
+            w_in = sb.tile([P, P * PACK], BF16, name=f"w_in{h}", align_bytes=64)
+            nc.scalar.copy(
+                w_in[:].bitcast(F32).rearrange("p (m u) -> p m u", u=2),
+                turned[:, 0 : 2 * P].rearrange("p (u m) -> p m u", u=2),
+            )
+            cols = slice(h * P, (h + 1) * P)
+            nc.vector.quantize_mx(out=w_codes[:, cols].bitcast(FP8X4), scales=w_scales[:, cols], in_=w_in[:])
+
+        taken(0)
+        taken(1)
+        values(0)
+        values(1)
+        p_all = sb.tile([P, QT, I], F32, name="p_all", tag="val_win1", align_bytes=64)
+        scores(0)
+        scores(1)
+        turn_values(0, "negs0")
+        damp(0)
+        turn_values(1, "negs1")
+        damp(1)
+        values(2)
+        weights(0)
+        values(3)
+        weights(1)
+        turn_values(2, "pos1")
+        turn_values(3, "v_in3")
+
+        y = [sb.tile([P, PACK, P], F32, name=f"y{h}", align_bytes=64) for h in range(QT)]
+        y_rows = out_0.rearrange("(p j) q -> p j q", j=PACK)
+
+        def finish(tag, planes, rows, off_engine):
+            n_rows = rows.stop - rows.start
+            width = len(planes) * n_rows
+            o = bank(tag)
+            for n, j in enumerate(planes):
+                cols = slice(j * P, (j + 1) * P)
+                nc.tensor.matmul_mx(
+                    out=o[:, n * n_rows : (n + 1) * n_rows],
+                    lhsT=v_codes[:, cols].bitcast(FP8X4), lhsT_scale=v_scales[:, cols],
+                    rhs=w_codes[:, rows].bitcast(FP8X4), rhs_scale=w_scales[:, rows], start=True, stop=True,
+                )
+            og = sb.tile([P, width // RUN], F32, name=f"og_{tag}")
+            nc.vector.tensor_reduce(og[:], o[:, 0:width].rearrange("p (k r) -> p k r", r=RUN), AX.X, ALU.add)
+            off = sb.tile([P, width], F32, name=f"off_{tag}", align_bytes=64)
+            groups = n_rows // RUN
+            off_engine.tensor_tensor(
+                off[:].rearrange("p (j k r) -> p j k r", k=groups, r=RUN),
+                hold_b[:, rows].rearrange("p (k r) -> p k r", r=RUN).unsqueeze(1).to_broadcast([P, len(planes), groups, RUN]),
+                og[:].rearrange("p (j k) -> p j k", k=groups).unsqueeze(3).to_broadcast([P, len(planes), groups, RUN]),
+                ALU.mult,
+            )
+            j0, j1 = planes[0], planes[-1] + 1
+            for h in range(rows.start // P, rows.stop // P):
+                cut = slice(h * P - rows.start, (h + 1) * P - rows.start)
+                nc.vector.tensor_tensor(
+                    y[h][:, j0:j1, :],
+                    o[:, 0:width].rearrange("p (j q) -> p j q", q=n_rows)[:, :, cut],
+                    off[:].rearrange("p (j q) -> p j q", q=n_rows)[:, :, cut],
+                    ALU.subtract,
+                )
+
+        finish("a0", [0, 1, 2], slice(0, P), nc.gpsimd)
+        finish("a1", [0, 1, 2], slice(P, Q), nc.gpsimd)
+        finish("b0", [3], slice(0, Q), nc.vector)
+
+        y_in = sb.tile([P, Q * PACK], BF16, name="y_in", align_bytes=64)
+        for h, copy in enumerate((nc.scalar.copy, nc.vector.tensor_copy)):
+            nc.sync.dma_start(y_rows[:, :, h * P : (h + 1) * P], y[h][:])
+            copy(
+                y_in[:, h * P * PACK : (h + 1) * P * PACK].rearrange("p (c i t) -> p c t i", i=4, t=PACK),
+                y[h][:].rearrange("p t (c i) -> p c t i", i=4),
+            )
+        y_codes = sb.tile([P, Q], U32, name="y_codes", align_bytes=64)
+        y_scales = sb.tile([P, Q], U8, name="y_scales", align_bytes=64)
+        nc.vector.quantize_mx(out=y_codes[:].bitcast(FP8X4), scales=y_scales[:], in_=y_in[:])
+        nc.sync.dma_start(out_1[0].rearrange("p c r -> p (c r)").bitcast(I32), y_codes[:].bitcast(I32))
+        for g in range(4):
+            eng = nc.scalar if g % 2 == 0 else nc.sync
+            eng.dma_start(out_2[0, 4 * g : 4 * g + 4, :].bitcast(I32), y_scales[32 * g : 32 * g + 4, :].bitcast(I32))

@@ -62,10 +62,11 @@ def tile_attend_withoutconcept_crowdshy_beyondgroupread_pl_kernel(
                 ks_win[32 * g : 32 * g + 4, :].bitcast(I32), keys_scales[0, 4 * g : 4 * g + 4, :].bitcast(I32)
             )
 
-        nc.sync.dma_start(hold_col[:], hold.rearrange("o (p e) -> p (o e)", e=QT))
         nc.sync.dma_start(idx2[:], offs2)
-        nc.sync.dma_start(idx[:], offs)
         nc.sync.dma_start(os_col[:], os_.rearrange("o (p t) -> p (o t)", t=PACK))
+        with nc.allow_non_contiguous_dma(reason="one value a partition"):
+            nc.sync.dma_start(hold_col[:], hold.rearrange("o (h p) -> p (o h)", p=P))
+        nc.sync.dma_start(idx[:], offs)
         nc.sync.dma_start(conc_win[0][:], conc_rows[0])
         nc.sync.dma_start(conc_win[1][:], conc_rows[1])
         load_scale_rows(nc.sync, 0)
@@ -86,22 +87,14 @@ def tile_attend_withoutconcept_crowdshy_beyondgroupread_pl_kernel(
         with nc.allow_non_contiguous_dma(reason="one value a partition"):
             nc.gpsimd.dma_start(shy_col[:], shy.rearrange("(h p) o -> p (h o)", p=P))
 
+        os_spread = bank("misc2")
+        for t in range(PACK):
+            nc.tensor.transpose(os_spread[:, t * P : (t + 1) * P], os_col[:, t : t + 1].to_broadcast([P, P]), ident[:])
         hold_8th = sb.tile([P, QT], F32, name="hold_8th")
         nc.scalar.activation(hold_8th[:], hold_col[:], ACT.Copy, scale=1.0 / RUN)
-        spread = bank("misc2")
-        for t in range(PACK):
-            nc.tensor.transpose(spread[:, t * P : (t + 1) * P], os_col[:, t : t + 1].to_broadcast([P, P]), ident[:])
-        os_b = sb.tile([P, I], F32, name="os_b", align_bytes=64)
-        nc.scalar.copy(os_b[:].rearrange("p (s t) -> p s t", t=PACK), spread[:].rearrange("p (t s) -> p s t", t=PACK))
-        spread = bank("misc3")
-        for e in range(QT):
-            nc.tensor.transpose(spread[:, e * P : (e + 1) * P], hold_8th[:, e : e + 1].to_broadcast([P, P]), ident[:])
-        hold_b = sb.tile([P, Q], F32, name="hold_b", align_bytes=64)
-        nc.scalar.copy(
-            hold_b[:].rearrange("p (s e) -> p s e", e=QT),
-            spread[:, 0:Q].rearrange("p (e s) -> p s e", e=QT),
-        )
-
+        hold_b = bank("misc3")
+        for h in range(QT):
+            nc.tensor.transpose(hold_b[:, h * P : (h + 1) * P], hold_8th[:, h : h + 1].to_broadcast([P, P]), ident[:])
         conc_g = sb.tile([P, PACK, I], BF16, name="conc_g", align_bytes=64)
 
         def gather(engine, out, window, offsets):
@@ -131,7 +124,7 @@ def tile_attend_withoutconcept_crowdshy_beyondgroupread_pl_kernel(
         part_spread = bank("misc1")
         for c in range(PACK):
             nc.tensor.transpose(part_spread[:, c * P : (c + 1) * P], part_col[:, c : c + 1].to_broadcast([P, P]), ident[:])
-        conc_in = sb.tile([P, I * PACK], BF16, name="conc_in", align_bytes=64)
+        conc_in = sb.tile([P, I * PACK], BF16, name="conc_in", tag="conc_in", align_bytes=64)
         nc.vector.tensor_copy(
             conc_in[:].rearrange("p (c i t) -> p c t i", i=4, t=PACK),
             conc_g[:].rearrange("p t (c i) -> p c t i", i=4),
@@ -141,19 +134,26 @@ def tile_attend_withoutconcept_crowdshy_beyondgroupread_pl_kernel(
         nc.vector.quantize_mx(out=c_codes[:].bitcast(FP8X4), scales=c_scales[:], in_=conc_in[:])
 
         q_in = sb.tile([P, Q * PACK], BF16, name="q_in", tag="q_in", align_bytes=64)
-        nc.scalar.copy(
-            q_in[:].rearrange("p (c i t) -> p c t i", i=4, t=PACK),
-            q_raw[:].rearrange("p t (c i) -> p c t i", i=4),
-        )
+        q_codes = sb.tile([P, Q], U32, name="q_codes", align_bytes=64)
+        q_scales = sb.tile([P, Q], U8, name="q_scales", align_bytes=64)
+        for h in range(QT):
+            rows, laid = slice(h * P, (h + 1) * P), slice(h * P * PACK, (h + 1) * P * PACK)
+            nc.scalar.copy(
+                q_in[:, laid].rearrange("p (c i t) -> p c t i", i=4, t=PACK),
+                q_raw[:, :, rows].rearrange("p t (c i) -> p c t i", i=4),
+            )
+            nc.vector.quantize_mx(out=q_codes[:, rows].bitcast(FP8X4), scales=q_scales[:, rows], in_=q_in[:, laid])
         part_b = sb.tile([P, I], F32, name="part_b", tag="q_raw", align_bytes=64)
         nc.scalar.copy(part_b[:], part_spread[:])
 
-        q_codes = sb.tile([P, Q], U32, name="q_codes", align_bytes=64)
-        q_scales = sb.tile([P, Q], U8, name="q_scales", align_bytes=64)
-        nc.vector.quantize_mx(out=q_codes[:].bitcast(FP8X4), scales=q_scales[:], in_=q_in[:])
+        spreads = sb.tile([P, I + P], F32, name="spreads", tag="q_in", align_bytes=64)
+        os_b = spreads[:, 0:I]
+        nc.scalar.copy(os_b.rearrange("p (s t) -> p s t", t=PACK), os_spread[:].rearrange("p (t s) -> p s t", t=PACK))
 
-        k_words = sb.tile([P, I], U16, name="k_words", tag="q_in", align_bytes=64)
-        nc.vector.tensor_copy(k_words[:], kw_win[:].indirect(idx[:]))
+        hold_sb = spreads[:, I:]
+        nc.scalar.copy(hold_sb, hold_b[:, 0:P])
+        k_words = sb.tile([P, I], U16, name="k_words", tag="conc_in", align_bytes=64)
+        gather_halves(["vector", "vector"], k_words, kw_win[:], idx)
 
         a_ps, b_ps = [], []
         for h in range(QT):
@@ -164,14 +164,15 @@ def tile_attend_withoutconcept_crowdshy_beyondgroupread_pl_kernel(
                 rhs=c_codes[:].bitcast(FP8X4), rhs_scale=c_scales[:], start=True, stop=True,
             )
             b_ps.append(b)
+        a_ps = [bank(f"a{h}") for h in range(QT)]
         for h in range(QT):
             cols = slice(h * P, (h + 1) * P)
-            a = bank(f"a{h}")
-            nc.tensor.matmul_mx(
-                out=a[:], lhsT=q_codes[:, cols].bitcast(FP8X4), lhsT_scale=q_scales[:, cols],
-                rhs=k_words[:].bitcast(FP4X4), rhs_scale=k_scales[:], start=True, stop=True,
-            )
-            a_ps.append(a)
+            for half in range(2):
+                slots = slice(half * I // 2, (half + 1) * I // 2)
+                nc.tensor.matmul_mx(
+                    out=a_ps[h][:, slots], lhsT=q_codes[:, cols].bitcast(FP8X4), lhsT_scale=q_scales[:, cols],
+                    rhs=k_words[:, slots].bitcast(FP4X4), rhs_scale=k_scales[:, slots], start=True, stop=True,
+                )
 
         v_codes = sb.tile([P, E], U32, name="v_codes", align_bytes=64)
         v_scales = sb.tile([P, E], U8, name="v_scales", align_bytes=64)
@@ -181,18 +182,16 @@ def tile_attend_withoutconcept_crowdshy_beyondgroupread_pl_kernel(
             gather_halves(([["scalar", "scalar"]] * 3 + [["scalar"]])[j], vg, val_win[j][:], idx)
             st["vg", j] = vg
 
-        def turn_values(j, tag):
-            pairs = st["vg", j][:].bitcast(F32)
-            turned = bank(f"misc{j % 2}")
+        def turn_pairs(turned, src):
+            pairs = src.bitcast(F32)
             for u in range(2):
                 nc.tensor.transpose(turned[:, u * P : (u + 1) * P], pairs[:, u : I // 2 : 2], ident[:])
-            v_in = sb.tile([P, P * PACK], BF16, name=f"v_in{j}", tag=tag, align_bytes=64)
+
+        def lay_out(dst, turned):
             nc.scalar.copy(
-                v_in[:].bitcast(F32).rearrange("p (m u) -> p m u", u=2),
-                turned[:, 0 : 2 * P].rearrange("p (u m) -> p m u", u=2),
+                dst.bitcast(F32).rearrange("p (n m u) -> p n m u", m=P, u=2),
+                turned.rearrange("p (n u m) -> p n m u", m=P, u=2),
             )
-            cols = slice(j * P, (j + 1) * P)
-            nc.vector.quantize_mx(out=v_codes[:, cols].bitcast(FP8X4), scales=v_scales[:, cols], in_=v_in[:])
 
         w_codes = sb.tile([P, Q], U32, name="w_codes", align_bytes=64)
         w_scales = sb.tile([P, Q], U8, name="w_scales", align_bytes=64)
@@ -222,8 +221,6 @@ def tile_attend_withoutconcept_crowdshy_beyondgroupread_pl_kernel(
 
         def damp(h):
             p, z = st["p", h], st["z", h]
-            pos = wide("pos", h)
-            nc.gpsimd.tensor_tensor(pos[:], p, os_b[:], ALU.mult)
             rz = small("rz", h)
             nc.vector.reciprocal(rz[:], z[:])
             pg = small("pg", h, I // RUN)
@@ -232,13 +229,22 @@ def tile_attend_withoutconcept_crowdshy_beyondgroupread_pl_kernel(
             nc.vector.tensor_scalar(c[:], rz[:], shy_col[:, h : h + 1], -1.0, ALU.mult, ALU.mult)
             k0 = small("k0", h, I // RUN)
             nc.scalar.activation(k0[:], pg[:], ACT.Exp, scale=c[:])
-            st["pos", h], st["pg", h], st["k0", h] = pos, pg, k0
+            st["pg", h], st["k0", h] = pg, k0
 
-        def weights(h):
-            pos, pg, k0 = st["pos", h], st["pg", h], st["k0", h]
+        def with_os(h, engine):
+            pos = wide("pos", h)
+            engine.tensor_tensor(pos[:], st["p", h], os_b, ALU.mult)
+            st["pos", h] = pos
+
+        def damped_sum(h):
+            pg, k0 = st["pg", h], st["k0", h]
             ug = small("ug", h, I // RUN)
             den = small("den", h)
             nc.vector.scalar_tensor_tensor(ug[:], pg[:], 1.0, k0[:], ALU.mult, ALU.mult, accum_out=den[:])
+            st["den", h] = den
+
+        def weights(h):
+            pos, k0, den = st["pos", h], st["k0", h], st["den", h]
             rden = small("rden", h)
             nc.vector.reciprocal(rden[:], den[:])
             wo = sb.tile([P, I], BF16, name=f"wo{h}", align_bytes=64)
@@ -249,17 +255,7 @@ def tile_attend_withoutconcept_crowdshy_beyondgroupread_pl_kernel(
                 k0[:].unsqueeze(2).to_broadcast([P, I // RUN, RUN]),
                 ALU.mult, ALU.mult,
             )
-            pairs = wo[:].bitcast(F32)
-            turned = bank(f"misc{2 + h}")
-            for u in range(2):
-                nc.tensor.transpose(turned[:, u * P : (u + 1) * P], pairs[:, u : I // 2 : 2], ident[:])
-            w_in = sb.tile([P, P * PACK], BF16, name=f"w_in{h}", align_bytes=64)
-            nc.scalar.copy(
-                w_in[:].bitcast(F32).rearrange("p (m u) -> p m u", u=2),
-                turned[:, 0 : 2 * P].rearrange("p (u m) -> p m u", u=2),
-            )
-            cols = slice(h * P, (h + 1) * P)
-            nc.vector.quantize_mx(out=w_codes[:, cols].bitcast(FP8X4), scales=w_scales[:, cols], in_=w_in[:])
+            st["wo", h] = wo
 
         taken(0)
         taken(1)
@@ -268,66 +264,98 @@ def tile_attend_withoutconcept_crowdshy_beyondgroupread_pl_kernel(
         p_all = sb.tile([P, QT, I], F32, name="p_all", tag="val_win1", align_bytes=64)
         scores(0)
         scores(1)
-        turn_values(0, "negs0")
+        with_os(0, nc.gpsimd)
         damp(0)
-        turn_values(1, "negs1")
         damp(1)
         values(2)
-        weights(0)
+        damped_sum(0)
+        with_os(1, nc.vector)
+        damped_sum(1)
         values(3)
+        weights(0)
         weights(1)
-        turn_values(2, "pos1")
-        turn_values(3, "v_in3")
+        W = P * PACK
+        v_in = sb.tile([P, 3 * W], BF16, name="v_in", tag="val_win3", align_bytes=64)
+        turned = bank("b1")
+        turn_pairs(turned[:, 0 : 2 * P], st["vg", 0][:])
+        turn_pairs(turned[:, 2 * P :], st["vg", 1][:])
+        lay_out(v_in[:, 0 : 2 * W], turned[:])
+        turned = bank("misc2")
+        turn_pairs(turned[:, 0 : 2 * P], st["vg", 2][:])
+        lay_out(v_in[:, 2 * W :], turned[:, 0 : 2 * P])
+        nc.vector.quantize_mx(out=v_codes[:, 0 : 3 * P].bitcast(FP8X4), scales=v_scales[:, 0 : 3 * P], in_=v_in[:])
+        turned = bank("misc0")
+        turn_pairs(turned[:, 0 : 2 * P], st["vg", 3][:])
+        turn_pairs(turned[:, 2 * P :], st["wo", 0][:])
+        w_in0 = sb.tile([P, W], BF16, name="w_in0", align_bytes=64)
+        lay_out(w_in0[:], turned[:, 2 * P :])
+        nc.vector.quantize_mx(out=w_codes[:, 0:P].bitcast(FP8X4), scales=w_scales[:, 0:P], in_=w_in0[:])
+        v_in3 = sb.tile([P, W], BF16, name="v_in3", align_bytes=64)
+        lay_out(v_in3[:], turned[:, 0 : 2 * P])
+        nc.vector.quantize_mx(out=v_codes[:, 3 * P :].bitcast(FP8X4), scales=v_scales[:, 3 * P :], in_=v_in3[:])
+        turned = bank("misc2")
+        turn_pairs(turned[:, 0 : 2 * P], st["wo", 1][:])
+        w_in1 = sb.tile([P, W], BF16, name="w_in1", align_bytes=64)
+        lay_out(w_in1[:], turned[:, 0 : 2 * P])
+        nc.vector.quantize_mx(out=w_codes[:, P:].bitcast(FP8X4), scales=w_scales[:, P:], in_=w_in1[:])
 
-        y = [sb.tile([P, PACK, P], F32, name=f"y{h}", align_bytes=64) for h in range(QT)]
         y_rows = out_0.rearrange("(p j) q -> p j q", j=PACK)
+        y_codes = sb.tile([P, Q], U32, name="y_codes", align_bytes=64)
+        y_scales = sb.tile([P, Q], U8, name="y_scales", align_bytes=64)
+        words_out = out_1[0].rearrange("p c r -> p (c r)").bitcast(I32)
+        groups = P // RUN
 
-        def finish(tag, planes, rows, off_engine):
-            n_rows = rows.stop - rows.start
-            width = len(planes) * n_rows
-            o = bank(tag)
-            for n, j in enumerate(planes):
-                cols = slice(j * P, (j + 1) * P)
+        o_banks = {(0, 0): "a0", (0, 1): "a1", (1, 0): "b0", (1, 1): "b1"}
+        y = [wide("y", h) for h in range(QT)]
+
+        def product(h, pair):
+            rows = slice(h * P, (h + 1) * P)
+            o = bank(o_banks[h, pair])
+            for n in range(2):
+                cols = slice((2 * pair + n) * P, (2 * pair + n + 1) * P)
                 nc.tensor.matmul_mx(
-                    out=o[:, n * n_rows : (n + 1) * n_rows],
+                    out=o[:, n * P : (n + 1) * P],
                     lhsT=v_codes[:, cols].bitcast(FP8X4), lhsT_scale=v_scales[:, cols],
                     rhs=w_codes[:, rows].bitcast(FP8X4), rhs_scale=w_scales[:, rows], start=True, stop=True,
                 )
-            og = sb.tile([P, width // RUN], F32, name=f"og_{tag}")
-            nc.vector.tensor_reduce(og[:], o[:, 0:width].rearrange("p (k r) -> p k r", r=RUN), AX.X, ALU.add)
-            off = sb.tile([P, width], F32, name=f"off_{tag}", align_bytes=64)
-            groups = n_rows // RUN
-            off_engine.tensor_tensor(
+            og = sb.tile([P, 2 * groups], F32, name=f"og{h}{pair}")
+            nc.vector.tensor_reduce(og[:], o[:, 0 : 2 * P].rearrange("p (k r) -> p k r", r=RUN), AX.X, ALU.add)
+            st["o", h, pair], st["og", h, pair] = o, og
+
+        def taken_off(h, pair):
+            rows = slice(h * P, (h + 1) * P)
+            og = st["og", h, pair]
+            off = sb.tile([P, 2 * P], F32, name=f"off{h}{pair}", align_bytes=64)
+            engine, factor = (nc.gpsimd, hold_sb) if h == 0 else (nc.vector, hold_b[:, rows])
+            engine.tensor_tensor(
                 off[:].rearrange("p (j k r) -> p j k r", k=groups, r=RUN),
-                hold_b[:, rows].rearrange("p (k r) -> p k r", r=RUN).unsqueeze(1).to_broadcast([P, len(planes), groups, RUN]),
-                og[:].rearrange("p (j k) -> p j k", k=groups).unsqueeze(3).to_broadcast([P, len(planes), groups, RUN]),
+                og[:].rearrange("p (j k) -> p j k", k=groups).unsqueeze(3).to_broadcast([P, 2, groups, RUN]),
+                factor.rearrange("p (k r) -> p k r", r=RUN).unsqueeze(1).to_broadcast([P, 2, groups, RUN]),
                 ALU.mult,
             )
-            j0, j1 = planes[0], planes[-1] + 1
-            for h in range(rows.start // P, rows.stop // P):
-                cut = slice(h * P - rows.start, (h + 1) * P - rows.start)
-                nc.vector.tensor_tensor(
-                    y[h][:, j0:j1, :],
-                    o[:, 0:width].rearrange("p (j q) -> p j q", q=n_rows)[:, :, cut],
-                    off[:].rearrange("p (j q) -> p j q", q=n_rows)[:, :, cut],
-                    ALU.subtract,
-                )
+            st["off", h, pair] = off
 
-        finish("a0", [0, 1, 2], slice(0, P), nc.gpsimd)
-        finish("a1", [0, 1, 2], slice(P, Q), nc.gpsimd)
-        finish("b0", [3], slice(0, Q), nc.vector)
+        def subtract(h, pair):
+            o, off = st["o", h, pair], st["off", h, pair]
+            nc.vector.tensor_tensor(y[h][:, 2 * pair * P : 2 * (pair + 1) * P], o[:, 0 : 2 * P], off[:], ALU.subtract)
 
-        y_in = sb.tile([P, Q * PACK], BF16, name="y_in", align_bytes=64)
-        for h, copy in enumerate((nc.scalar.copy, nc.vector.tensor_copy)):
-            nc.sync.dma_start(y_rows[:, :, h * P : (h + 1) * P], y[h][:])
+        def finish(h, copy):
+            rows = slice(h * P, (h + 1) * P)
+            nc.sync.dma_start(y_rows[:, :, rows], y[h][:].rearrange("p (j q) -> p j q", j=PACK))
             copy(
                 y_in[:, h * P * PACK : (h + 1) * P * PACK].rearrange("p (c i t) -> p c t i", i=4, t=PACK),
-                y[h][:].rearrange("p t (c i) -> p c t i", i=4),
+                y[h][:].rearrange("p (t c i) -> p c t i", i=4, t=PACK),
             )
-        y_codes = sb.tile([P, Q], U32, name="y_codes", align_bytes=64)
-        y_scales = sb.tile([P, Q], U8, name="y_scales", align_bytes=64)
+
+        units = [(h, pair) for h in range(QT) for pair in range(2)]
+        for step in (product, taken_off, subtract):
+            for unit in units:
+                step(*unit)
+        y_in = sb.tile([P, Q * PACK], BF16, name="y_in", align_bytes=64)
+        finish(0, nc.scalar.copy)
+        finish(1, nc.vector.tensor_copy)
         nc.vector.quantize_mx(out=y_codes[:].bitcast(FP8X4), scales=y_scales[:], in_=y_in[:])
-        nc.sync.dma_start(out_1[0].rearrange("p c r -> p (c r)").bitcast(I32), y_codes[:].bitcast(I32))
+        nc.sync.dma_start(words_out, y_codes[:].bitcast(I32))
         for g in range(4):
             eng = nc.scalar if g % 2 == 0 else nc.sync
             eng.dma_start(out_2[0, 4 * g : 4 * g + 4, :].bitcast(I32), y_scales[32 * g : 32 * g + 4, :].bitcast(I32))

@@ -35,6 +35,12 @@ def tile_attend_withoutconcept_crowdshy_beyondgroupread_pl_kernel(
         def bank(tag):
             return ps.tile([P, 512], F32, name=tag, tag=tag)
 
+        def dealt(ap):
+            return ap.rearrange("p (u s e) -> p u s e", u=2, e=2)
+
+        def in_slot_order(ap):
+            return ap.rearrange("p (s u e) -> p u s e", u=2, e=2)
+
         ks_win = sb.tile([P, T], U8, name="ks_win", align_bytes=64)
         nc.gpsimd.memset(ks_win[:].bitcast(I32), 0)
         part_win = sb.tile([P, T], F32, name="part_win", align_bytes=64)
@@ -80,10 +86,10 @@ def tile_attend_withoutconcept_crowdshy_beyondgroupread_pl_kernel(
         nc.sync.dma_start(kw_win[:].bitcast(I32), keys_words[0].bitcast(I32))
         nc.sync.dma_start(val_win[0][:], val_rows[0])
         nc.sync.dma_start(val_win[1][:], val_rows[1])
+        with nc.allow_non_contiguous_dma(reason="one value a partition"):
+            nc.sync.dma_start(lam_col[:], lam.rearrange("(h p) o -> p (h o)", p=P))
         nc.sync.dma_start(val_win[2][:], val_rows[2])
         nc.sync.dma_start(val_win[3][:], val_rows[3])
-        with nc.allow_non_contiguous_dma(reason="one value a partition"):
-            nc.gpsimd.dma_start(lam_col[:], lam.rearrange("(h p) o -> p (h o)", p=P))
         with nc.allow_non_contiguous_dma(reason="one value a partition"):
             nc.gpsimd.dma_start(shy_col[:], shy.rearrange("(h p) o -> p (h o)", p=P))
 
@@ -144,14 +150,14 @@ def tile_attend_withoutconcept_crowdshy_beyondgroupread_pl_kernel(
             )
             nc.vector.quantize_mx(out=q_codes[:, rows].bitcast(FP8X4), scales=q_scales[:, rows], in_=q_in[:, laid])
         part_b = sb.tile([P, I], F32, name="part_b", tag="q_raw", align_bytes=64)
-        nc.scalar.copy(part_b[:], part_spread[:])
+        nc.scalar.copy(dealt(part_b[:]), in_slot_order(part_spread[:]))
 
-        spreads = sb.tile([P, I + P], F32, name="spreads", tag="q_in", align_bytes=64)
+        spreads = sb.tile([P, I + Q], F32, name="spreads", tag="q_in", align_bytes=64)
         os_b = spreads[:, 0:I]
-        nc.scalar.copy(os_b.rearrange("p (s t) -> p s t", t=PACK), os_spread[:].rearrange("p (t s) -> p s t", t=PACK))
+        nc.scalar.copy(dealt(os_b), os_spread[:].rearrange("p (u e s) -> p u s e", u=2, e=2))
 
         hold_sb = spreads[:, I:]
-        nc.scalar.copy(hold_sb, hold_b[:, 0:P])
+        nc.scalar.copy(hold_sb, hold_b[:, 0:Q])
         k_words = sb.tile([P, I], U16, name="k_words", tag="conc_in", align_bytes=64)
         gather_halves(["vector", "vector"], k_words, kw_win[:], idx)
 
@@ -187,8 +193,8 @@ def tile_attend_withoutconcept_crowdshy_beyondgroupread_pl_kernel(
             for u in range(2):
                 nc.tensor.transpose(turned[:, u * P : (u + 1) * P], pairs[:, u : I // 2 : 2], ident[:])
 
-        def lay_out(dst, turned):
-            nc.scalar.copy(
+        def lay_out(copy, dst, turned):
+            copy(
                 dst.bitcast(F32).rearrange("p (n m u) -> p n m u", m=P, u=2),
                 turned.rearrange("p (n u m) -> p n m u", m=P, u=2),
             )
@@ -205,12 +211,12 @@ def tile_attend_withoutconcept_crowdshy_beyondgroupread_pl_kernel(
 
         def taken(h):
             t = wide("taken", h)
-            nc.vector.tensor_tensor(t[:], b_ps[h][:], part_b[:], ALU.mult)
+            nc.vector.tensor_tensor(dealt(t[:]), in_slot_order(b_ps[h][:]), dealt(part_b[:]), ALU.mult)
             st["t", h] = t
 
         def scores(h):
             d = wide("diff", h)
-            nc.vector.tensor_tensor(d[:], st["t", h][:], a_ps[h][:], ALU.subtract)
+            nc.vector.tensor_tensor(dealt(d[:]), dealt(st["t", h][:]), in_slot_order(a_ps[h][:]), ALU.subtract)
             ns = wide("negs", h)
             mn = small("mn", h)
             nc.vector.tensor_scalar(ns[:], d[:], lam_col[:, h : h + 1], None, ALU.mult, ALU.min, accum_out=mn[:])
@@ -224,7 +230,7 @@ def tile_attend_withoutconcept_crowdshy_beyondgroupread_pl_kernel(
             rz = small("rz", h)
             nc.vector.reciprocal(rz[:], z[:])
             pg = small("pg", h, I // RUN)
-            nc.vector.tensor_reduce(pg[:], p.rearrange("p (g r) -> p g r", r=RUN), AX.X, ALU.add)
+            nc.vector.tensor_reduce(pg[:], p.rearrange("p (u g r) -> p g u r", u=2, r=RUN // 2), AX.XY, ALU.add)
             c = small("c", h)
             nc.vector.tensor_scalar(c[:], rz[:], shy_col[:, h : h + 1], -1.0, ALU.mult, ALU.mult)
             k0 = small("k0", h, I // RUN)
@@ -248,56 +254,59 @@ def tile_attend_withoutconcept_crowdshy_beyondgroupread_pl_kernel(
             rden = small("rden", h)
             nc.vector.reciprocal(rden[:], den[:])
             wo = sb.tile([P, I], BF16, name=f"wo{h}", align_bytes=64)
-            nc.vector.scalar_tensor_tensor(
-                wo[:].rearrange("p (g r) -> p g r", r=RUN),
-                pos[:].rearrange("p (g r) -> p g r", r=RUN),
-                rden[:],
-                k0[:].unsqueeze(2).to_broadcast([P, I // RUN, RUN]),
-                ALU.mult, ALU.mult,
-            )
-            st["wo", h] = wo
+            turned = bank(f"misc{h}")
+            for u in range(2):
+                half = slice(u * I // 2, (u + 1) * I // 2)
+                nc.vector.scalar_tensor_tensor(
+                    wo[:, half].rearrange("p (g r) -> p g r", r=RUN // 2),
+                    pos[:, half].rearrange("p (g r) -> p g r", r=RUN // 2),
+                    rden[:],
+                    k0[:].unsqueeze(2).to_broadcast([P, I // RUN, RUN // 2]),
+                    ALU.mult, ALU.mult,
+                )
+                nc.tensor.transpose(turned[:, u * P : (u + 1) * P], wo[:, half].bitcast(F32), ident[:])
+            st["turned", h] = turned
 
         taken(0)
         taken(1)
         values(0)
         values(1)
-        p_all = sb.tile([P, QT, I], F32, name="p_all", tag="val_win1", align_bytes=64)
+        p_all = sb.tile([P, QT, I], F32, name="p_all", align_bytes=64)
         scores(0)
         scores(1)
+        W = P * PACK
+        turned01 = bank("b1")
+        turn_pairs(turned01[:, 0 : 2 * P], st["vg", 0][:])
+        v_in0 = sb.tile([P, W], BF16, name="v_in0", tag="diff0", align_bytes=64)
+        lay_out(nc.vector.tensor_copy, v_in0[:], turned01[:, 0 : 2 * P])
+        turned12 = bank("misc2")
+        turn_pairs(turned12[:, 0 : 2 * P], st["vg", 1][:])
         with_os(0, nc.gpsimd)
         damp(0)
         damp(1)
         values(2)
+        turn_pairs(turned12[:, 2 * P :], st["vg", 2][:])
         damped_sum(0)
         with_os(1, nc.vector)
         damped_sum(1)
         values(3)
         weights(0)
         weights(1)
-        W = P * PACK
-        v_in = sb.tile([P, 3 * W], BF16, name="v_in", tag="val_win3", align_bytes=64)
-        turned = bank("b1")
-        turn_pairs(turned[:, 0 : 2 * P], st["vg", 0][:])
-        turn_pairs(turned[:, 2 * P :], st["vg", 1][:])
-        lay_out(v_in[:, 0 : 2 * W], turned[:])
-        turned = bank("misc2")
-        turn_pairs(turned[:, 0 : 2 * P], st["vg", 2][:])
-        lay_out(v_in[:, 2 * W :], turned[:, 0 : 2 * P])
-        nc.vector.quantize_mx(out=v_codes[:, 0 : 3 * P].bitcast(FP8X4), scales=v_scales[:, 0 : 3 * P], in_=v_in[:])
-        turned = bank("misc0")
-        turn_pairs(turned[:, 0 : 2 * P], st["vg", 3][:])
-        turn_pairs(turned[:, 2 * P :], st["wo", 0][:])
-        w_in0 = sb.tile([P, W], BF16, name="w_in0", align_bytes=64)
-        lay_out(w_in0[:], turned[:, 2 * P :])
+        v_in12 = sb.tile([P, 2 * W], BF16, name="v_in12", tag="pos1", align_bytes=64)
+        lay_out(nc.vector.tensor_copy, v_in12[:], turned12[:])
+        nc.vector.quantize_mx(out=v_codes[:, 0:P].bitcast(FP8X4), scales=v_scales[:, 0:P], in_=v_in0[:])
+        w_in0 = sb.tile([P, W], BF16, name="w_in0", tag="val_win3", align_bytes=64)
+        lay_out(nc.scalar.copy, w_in0[:], st["turned", 0][:, 0 : 2 * P])
         nc.vector.quantize_mx(out=w_codes[:, 0:P].bitcast(FP8X4), scales=w_scales[:, 0:P], in_=w_in0[:])
-        v_in3 = sb.tile([P, W], BF16, name="v_in3", align_bytes=64)
-        lay_out(v_in3[:], turned[:, 0 : 2 * P])
-        nc.vector.quantize_mx(out=v_codes[:, 3 * P :].bitcast(FP8X4), scales=v_scales[:, 3 * P :], in_=v_in3[:])
-        turned = bank("misc2")
-        turn_pairs(turned[:, 0 : 2 * P], st["wo", 1][:])
+        nc.vector.quantize_mx(out=v_codes[:, P : 3 * P].bitcast(FP8X4), scales=v_scales[:, P : 3 * P], in_=v_in12[:])
         w_in1 = sb.tile([P, W], BF16, name="w_in1", align_bytes=64)
-        lay_out(w_in1[:], turned[:, 0 : 2 * P])
+        lay_out(nc.scalar.copy, w_in1[:], st["turned", 1][:, 0 : 2 * P])
         nc.vector.quantize_mx(out=w_codes[:, P:].bitcast(FP8X4), scales=w_scales[:, P:], in_=w_in1[:])
+        turned3 = bank("b0")
+        turn_pairs(turned3[:, 0 : 2 * P], st["vg", 3][:])
+        v_in3 = sb.tile([P, W], BF16, name="v_in3", align_bytes=64)
+        lay_out(nc.scalar.copy, v_in3[:], turned3[:, 0 : 2 * P])
+        nc.vector.quantize_mx(out=v_codes[:, 3 * P :].bitcast(FP8X4), scales=v_scales[:, 3 * P :], in_=v_in3[:])
 
         y_rows = out_0.rearrange("(p j) q -> p j q", j=PACK)
         y_codes = sb.tile([P, Q], U32, name="y_codes", align_bytes=64)
@@ -305,7 +314,7 @@ def tile_attend_withoutconcept_crowdshy_beyondgroupread_pl_kernel(
         words_out = out_1[0].rearrange("p c r -> p (c r)").bitcast(I32)
         groups = P // RUN
 
-        o_banks = {(0, 0): "a0", (0, 1): "a1", (1, 0): "b0", (1, 1): "b1"}
+        o_banks = {(0, 0): "a0", (0, 1): "a1", (1, 0): "b1", (1, 1): "misc2"}
         y = [wide("y", h) for h in range(QT)]
 
         def product(h, pair):
@@ -326,7 +335,7 @@ def tile_attend_withoutconcept_crowdshy_beyondgroupread_pl_kernel(
             rows = slice(h * P, (h + 1) * P)
             og = st["og", h, pair]
             off = sb.tile([P, 2 * P], F32, name=f"off{h}{pair}", align_bytes=64)
-            engine, factor = (nc.gpsimd, hold_sb) if h == 0 else (nc.vector, hold_b[:, rows])
+            engine, factor = (nc.vector, hold_b[:, rows]) if pair == 1 else (nc.gpsimd, hold_sb[:, rows])
             engine.tensor_tensor(
                 off[:].rearrange("p (j k r) -> p j k r", k=groups, r=RUN),
                 og[:].rearrange("p (j k) -> p j k", k=groups).unsqueeze(3).to_broadcast([P, 2, groups, RUN]),
@@ -347,7 +356,7 @@ def tile_attend_withoutconcept_crowdshy_beyondgroupread_pl_kernel(
                 y[h][:].rearrange("p (t c i) -> p c t i", i=4, t=PACK),
             )
 
-        units = [(h, pair) for h in range(QT) for pair in range(2)]
+        units = [(h, pair) for pair in range(2) for h in range(QT)]
         for step in (product, taken_off, subtract):
             for unit in units:
                 step(*unit)

@@ -70,8 +70,7 @@ def tile_attend_withoutconcept_crowdshy_beyondgroupread_pl_kernel(
 
         nc.sync.dma_start(idx2[:], offs2)
         nc.sync.dma_start(os_col[:], os_.rearrange("o (p t) -> p (o t)", t=PACK))
-        with nc.allow_non_contiguous_dma(reason="one value a partition"):
-            nc.sync.dma_start(hold_col[:], hold.rearrange("o (h p) -> p (o h)", p=P))
+        nc.sync.dma_start(hold_col[:], hold.rearrange("o (p e) -> p (o e)", e=QT))
         nc.sync.dma_start(idx[:], offs)
         nc.sync.dma_start(conc_win[0][:], conc_rows[0])
         nc.sync.dma_start(conc_win[1][:], conc_rows[1])
@@ -86,10 +85,10 @@ def tile_attend_withoutconcept_crowdshy_beyondgroupread_pl_kernel(
         nc.sync.dma_start(kw_win[:].bitcast(I32), keys_words[0].bitcast(I32))
         nc.sync.dma_start(val_win[0][:], val_rows[0])
         nc.sync.dma_start(val_win[1][:], val_rows[1])
-        with nc.allow_non_contiguous_dma(reason="one value a partition"):
-            nc.sync.dma_start(lam_col[:], lam.rearrange("(h p) o -> p (h o)", p=P))
         nc.sync.dma_start(val_win[2][:], val_rows[2])
         nc.sync.dma_start(val_win[3][:], val_rows[3])
+        with nc.allow_non_contiguous_dma(reason="one value a partition"):
+            nc.gpsimd.dma_start(lam_col[:], lam.rearrange("(h p) o -> p (h o)", p=P))
         with nc.allow_non_contiguous_dma(reason="one value a partition"):
             nc.gpsimd.dma_start(shy_col[:], shy.rearrange("(h p) o -> p (h o)", p=P))
 
@@ -100,7 +99,7 @@ def tile_attend_withoutconcept_crowdshy_beyondgroupread_pl_kernel(
         nc.scalar.activation(hold_8th[:], hold_col[:], ACT.Copy, scale=1.0 / RUN)
         hold_b = bank("misc3")
         for h in range(QT):
-            nc.tensor.transpose(hold_b[:, h * P : (h + 1) * P], hold_8th[:, h : h + 1].to_broadcast([P, P]), ident[:])
+            nc.tensor.transpose(hold_b[:, h:Q:QT], hold_8th[:, h : h + 1].to_broadcast([P, P]), ident[:])
         conc_g = sb.tile([P, PACK, I], BF16, name="conc_g", align_bytes=64)
 
         def gather(engine, out, window, offsets):
@@ -180,12 +179,11 @@ def tile_attend_withoutconcept_crowdshy_beyondgroupread_pl_kernel(
                     rhs=k_words[:, slots].bitcast(FP4X4), rhs_scale=k_scales[:, slots], start=True, stop=True,
                 )
 
-        v_codes = sb.tile([P, E], U32, name="v_codes", align_bytes=64)
         v_scales = sb.tile([P, E], U8, name="v_scales", align_bytes=64)
 
         def values(j):
             vg = sb.tile([P, I], BF16, name=f"val_g{j}", align_bytes=64)
-            gather_halves(([["scalar", "scalar"]] * 3 + [["scalar"]])[j], vg, val_win[j][:], idx)
+            gather_halves(([["scalar"]] * 4)[j], vg, val_win[j][:], idx)
             st["vg", j] = vg
 
         def turn_pairs(turned, src):
@@ -233,9 +231,7 @@ def tile_attend_withoutconcept_crowdshy_beyondgroupread_pl_kernel(
             nc.vector.tensor_reduce(pg[:], p.rearrange("p (u g r) -> p g u r", u=2, r=RUN // 2), AX.XY, ALU.add)
             c = small("c", h)
             nc.vector.tensor_scalar(c[:], rz[:], shy_col[:, h : h + 1], -1.0, ALU.mult, ALU.mult)
-            k0 = small("k0", h, I // RUN)
-            nc.scalar.activation(k0[:], pg[:], ACT.Exp, scale=c[:])
-            st["pg", h], st["k0", h] = pg, k0
+            st["pg", h], st["c", h] = pg, c
 
         def with_os(h, engine):
             pos = wide("pos", h)
@@ -243,16 +239,14 @@ def tile_attend_withoutconcept_crowdshy_beyondgroupread_pl_kernel(
             st["pos", h] = pos
 
         def damped_sum(h):
-            pg, k0 = st["pg", h], st["k0", h]
+            pg, k0 = st["pg", h], k0_all[:, h, :]
+            nc.scalar.activation(k0, pg[:], ACT.Exp, scale=st["c", h][:])
+            st["k0", h] = k0
             ug = small("ug", h, I // RUN)
-            den = small("den", h)
-            nc.vector.scalar_tensor_tensor(ug[:], pg[:], 1.0, k0[:], ALU.mult, ALU.mult, accum_out=den[:])
-            st["den", h] = den
+            nc.vector.scalar_tensor_tensor(ug[:], pg[:], 1.0, k0, ALU.mult, ALU.mult, accum_out=den[:, h : h + 1])
 
         def weights(h):
-            pos, k0, den = st["pos", h], st["k0", h], st["den", h]
-            rden = small("rden", h)
-            nc.vector.reciprocal(rden[:], den[:])
+            pos, k0 = st["pos", h], st["k0", h]
             wo = sb.tile([P, I], BF16, name=f"wo{h}", align_bytes=64)
             turned = bank(f"misc{h}")
             for u in range(2):
@@ -260,8 +254,8 @@ def tile_attend_withoutconcept_crowdshy_beyondgroupread_pl_kernel(
                 nc.vector.scalar_tensor_tensor(
                     wo[:, half].rearrange("p (g r) -> p g r", r=RUN // 2),
                     pos[:, half].rearrange("p (g r) -> p g r", r=RUN // 2),
-                    rden[:],
-                    k0[:].unsqueeze(2).to_broadcast([P, I // RUN, RUN // 2]),
+                    rden[:, h : h + 1],
+                    k0.unsqueeze(2).to_broadcast([P, I // RUN, RUN // 2]),
                     ALU.mult, ALU.mult,
                 )
                 nc.tensor.transpose(turned[:, u * P : (u + 1) * P], wo[:, half].bitcast(F32), ident[:])
@@ -271,34 +265,36 @@ def tile_attend_withoutconcept_crowdshy_beyondgroupread_pl_kernel(
         taken(1)
         values(0)
         values(1)
-        p_all = sb.tile([P, QT, I], F32, name="p_all", align_bytes=64)
+        p_all = sb.tile([P, QT, I], F32, name="p_all", tag="val_win1", align_bytes=64)
         scores(0)
         scores(1)
         W = P * PACK
         turned01 = bank("b1")
         turn_pairs(turned01[:, 0 : 2 * P], st["vg", 0][:])
-        v_in0 = sb.tile([P, W], BF16, name="v_in0", tag="diff0", align_bytes=64)
-        lay_out(nc.vector.tensor_copy, v_in0[:], turned01[:, 0 : 2 * P])
-        turned12 = bank("misc2")
-        turn_pairs(turned12[:, 0 : 2 * P], st["vg", 1][:])
+        turn_pairs(turned01[:, 2 * P :], st["vg", 1][:])
         with_os(0, nc.gpsimd)
         damp(0)
         damp(1)
         values(2)
-        turn_pairs(turned12[:, 2 * P :], st["vg", 2][:])
-        damped_sum(0)
+        turned2 = bank("misc2")
+        turn_pairs(turned2[:, 0 : 2 * P], st["vg", 2][:])
+        k0_all = sb.tile([P, QT, I // RUN], F32, name="k0_all", tag="val_win2", align_bytes=64)
+        den = small("den", "", QT)
         with_os(1, nc.vector)
+        damped_sum(0)
         damped_sum(1)
         values(3)
+        v_codes = sb.tile([P, E], U32, name="v_codes", align_bytes=64)
+        rden = small("rden", "", QT)
+        nc.vector.reciprocal(rden[:], den[:])
         weights(0)
         weights(1)
-        v_in12 = sb.tile([P, 2 * W], BF16, name="v_in12", tag="pos1", align_bytes=64)
-        lay_out(nc.vector.tensor_copy, v_in12[:], turned12[:])
-        nc.vector.quantize_mx(out=v_codes[:, 0:P].bitcast(FP8X4), scales=v_scales[:, 0:P], in_=v_in0[:])
-        w_in0 = sb.tile([P, W], BF16, name="w_in0", tag="val_win3", align_bytes=64)
-        lay_out(nc.scalar.copy, w_in0[:], st["turned", 0][:, 0 : 2 * P])
-        nc.vector.quantize_mx(out=w_codes[:, 0:P].bitcast(FP8X4), scales=w_scales[:, 0:P], in_=w_in0[:])
-        nc.vector.quantize_mx(out=v_codes[:, P : 3 * P].bitcast(FP8X4), scales=v_scales[:, P : 3 * P], in_=v_in12[:])
+        laid = sb.tile([P, 4 * W], BF16, name="laid", tag="val_win3", align_bytes=64)
+        lay_out(nc.scalar.copy, laid[:, 0 : 2 * W], turned01[:])
+        lay_out(nc.scalar.copy, laid[:, 2 * W : 3 * W], turned2[:, 0 : 2 * P])
+        nc.vector.quantize_mx(out=v_codes[:, 0 : 3 * P].bitcast(FP8X4), scales=v_scales[:, 0 : 3 * P], in_=laid[:, 0 : 3 * W])
+        lay_out(nc.scalar.copy, laid[:, 3 * W :], st["turned", 0][:, 0 : 2 * P])
+        nc.vector.quantize_mx(out=w_codes[:, 0:P].bitcast(FP8X4), scales=w_scales[:, 0:P], in_=laid[:, 3 * W :])
         w_in1 = sb.tile([P, W], BF16, name="w_in1", align_bytes=64)
         lay_out(nc.scalar.copy, w_in1[:], st["turned", 1][:, 0 : 2 * P])
         nc.vector.quantize_mx(out=w_codes[:, P:].bitcast(FP8X4), scales=w_scales[:, P:], in_=w_in1[:])

@@ -49,8 +49,8 @@ def tile_attend_withoutconcept_crowdshy_beyondgroupread_pl_kernel(
         make_identity(nc, ident[:])
         nc.gpsimd.memset(part_win[:, T // 2 : T], 0.0)
 
-        lam_col = sb.tile([P, QT], F32, name="lam_col")
-        shy_col = sb.tile([P, QT], F32, name="shy_col")
+        row_factors = sb.tile([P, Q], F32, name="row_factors", align_bytes=64)
+        nc.gpsimd.memset(row_factors[:], 0.0)
         os_col = sb.tile([P, PACK], F32, name="os_col")
         hold_col = sb.tile([P, QT], F32, name="hold_col")
 
@@ -65,7 +65,7 @@ def tile_attend_withoutconcept_crowdshy_beyondgroupread_pl_kernel(
 
         def load_scale_rows(queue, g):
             queue.dma_start(
-                ks_win[32 * g : 32 * g + 4, :].bitcast(I32), keys_scales[0, 4 * g : 4 * g + 4, :].bitcast(I32)
+                ks_win[g:P:32, :].bitcast(I32), keys_scales[0, g:16:4, :].bitcast(I32)
             )
 
         nc.sync.dma_start(idx2[:], offs2)
@@ -81,16 +81,14 @@ def tile_attend_withoutconcept_crowdshy_beyondgroupread_pl_kernel(
         load_scale_rows(nc.sync, 3)
         nc.sync.dma_start(conc_win[2][:], conc_rows[2])
         nc.sync.dma_start(conc_win[3][:], conc_rows[3])
+        nc.sync.dma_start(row_factors[0:1, :], lam.rearrange("q o -> o q"))
+        nc.sync.dma_start(row_factors[1:2, :], shy.rearrange("q o -> o q"))
         nc.sync.dma_start(q_raw[:], query.rearrange("(p t) q -> p t q", t=PACK))
         nc.sync.dma_start(kw_win[:].bitcast(I32), keys_words[0].bitcast(I32))
         nc.sync.dma_start(val_win[0][:], val_rows[0])
         nc.sync.dma_start(val_win[1][:], val_rows[1])
         nc.sync.dma_start(val_win[2][:], val_rows[2])
         nc.sync.dma_start(val_win[3][:], val_rows[3])
-        with nc.allow_non_contiguous_dma(reason="one value a partition"):
-            nc.gpsimd.dma_start(lam_col[:], lam.rearrange("(h p) o -> p (h o)", p=P))
-        with nc.allow_non_contiguous_dma(reason="one value a partition"):
-            nc.gpsimd.dma_start(shy_col[:], shy.rearrange("(h p) o -> p (h o)", p=P))
 
         os_spread = bank("misc2")
         for t in range(PACK):
@@ -151,12 +149,17 @@ def tile_attend_withoutconcept_crowdshy_beyondgroupread_pl_kernel(
         part_b = sb.tile([P, I], F32, name="part_b", tag="q_raw", align_bytes=64)
         nc.scalar.copy(dealt(part_b[:]), in_slot_order(part_spread[:]))
 
-        spreads = sb.tile([P, I + Q], F32, name="spreads", tag="q_in", align_bytes=64)
+        spreads = sb.tile([P, I + Q + 2 * QT], F32, name="spreads", tag="q_in", align_bytes=64)
         os_b = spreads[:, 0:I]
         nc.scalar.copy(dealt(os_b), os_spread[:].rearrange("p (u e s) -> p u s e", u=2, e=2))
 
-        hold_sb = spreads[:, I:]
+        hold_sb = spreads[:, I : I + Q]
         nc.scalar.copy(hold_sb, hold_b[:, 0:Q])
+        turned_rows = bank("misc0")
+        for h in range(QT):
+            nc.tensor.transpose(turned_rows[:, h * P : (h + 1) * P], row_factors[:, h * P : (h + 1) * P], ident[:])
+        factors = spreads[:, I + Q :].rearrange("p (h n) -> p h n", n=2)
+        nc.scalar.copy(factors, turned_rows[:, 0:Q].rearrange("p (h n) -> p h n", n=P)[:, :, 0:2])
         k_words = sb.tile([P, I], U16, name="k_words", tag="conc_in", align_bytes=64)
         gather_halves(["vector", "vector"], k_words, kw_win[:], idx)
 
@@ -217,7 +220,7 @@ def tile_attend_withoutconcept_crowdshy_beyondgroupread_pl_kernel(
             nc.vector.tensor_tensor(dealt(d[:]), dealt(st["t", h][:]), in_slot_order(a_ps[h][:]), ALU.subtract)
             ns = wide("negs", h)
             mn = small("mn", h)
-            nc.vector.tensor_scalar(ns[:], d[:], lam_col[:, h : h + 1], None, ALU.mult, ALU.min, accum_out=mn[:])
+            nc.vector.tensor_scalar(ns[:], d[:], factors[:, h, 0:1], None, ALU.mult, ALU.min, accum_out=mn[:])
             p = p_all[:, h, :]
             z = small("z", h)
             nc.scalar.activation(p, ns[:], ACT.Exp, bias=mn[:], scale=-1.0, accum_out=z[:])
@@ -230,7 +233,7 @@ def tile_attend_withoutconcept_crowdshy_beyondgroupread_pl_kernel(
             pg = small("pg", h, I // RUN)
             nc.vector.tensor_reduce(pg[:], p.rearrange("p (u g r) -> p g u r", u=2, r=RUN // 2), AX.XY, ALU.add)
             c = small("c", h)
-            nc.vector.tensor_scalar(c[:], rz[:], shy_col[:, h : h + 1], -1.0, ALU.mult, ALU.mult)
+            nc.vector.tensor_scalar(c[:], rz[:], factors[:, h, 1:2], -1.0, ALU.mult, ALU.mult)
             st["pg", h], st["c", h] = pg, c
 
         def with_os(h, engine):

from contextlib import ExitStack

import concourse.mybir as mybir
from concourse.masks import make_identity

F32 = mybir.dt.float32
BF16 = mybir.dt.bfloat16
I32 = mybir.dt.int32
U32 = mybir.dt.uint32
U16 = mybir.dt.uint16
U8 = mybir.dt.uint8
FP8X4 = mybir.dt.float8_e4m3fn_x4
FP4X4 = mybir.dt.float4_e2m1fn_x4
ALU = mybir.AluOpType
ACT = mybir.ActivationFunctionType
AX = mybir.AxisListType

P = 128
PACK = 4
D, T, I, Q, E, U = 512, 2048, 512, 256, 512, 1024
RUN = 8
QT = Q // P

FLOPS = 2 * D * Q * I * 2 + 2 * I * E * Q


def tile_attend_withoutconcept_crowdshy_beyondgroupread_pl_kernel(
    tc, query, keys_words, keys_scales, concepts, part, lam, shy, os_, vals, hold, offs, offs2, out_0, out_1, out_2
):
    nc = tc.nc
    with ExitStack() as ctx:
        sb = ctx.enter_context(tc.tile_pool(name="sb", bufs=1))
        ps = ctx.enter_context(tc.psum_pool(name="ps", bufs=1))

        def bank(tag):
            return ps.tile([P, 512], F32, name=tag, tag=tag)

        def dealt(ap):
            return ap.rearrange("p (u s e) -> p u s e", u=2, e=2)

        def in_slot_order(ap):
            return ap.rearrange("p (s u e) -> p u s e", u=2, e=2)

        ks_win = sb.tile([P, T], U8, name="ks_win", align_bytes=64)
        nc.gpsimd.memset(ks_win[:].bitcast(I32), 0)
        part_win = sb.tile([P, T], F32, name="part_win", align_bytes=64)
        nc.vector.memset(part_win[:, 0 : T // 2], 0.0)
        ident = sb.tile([P, P], F32, name="ident", align_bytes=64)
        make_identity(nc, ident[:])
        nc.gpsimd.memset(part_win[:, T // 2 : T], 0.0)

        row_factors = sb.tile([P, Q], F32, name="row_factors", align_bytes=64)
        nc.gpsimd.memset(row_factors[:], 0.0)
        os_col = sb.tile([P, PACK], F32, name="os_col")
        hold_col = sb.tile([P, QT], F32, name="hold_col")

        conc_rows = concepts.rearrange("(p t) u -> t p u", t=PACK)
        conc_win = [sb.tile([P, U], F32, name=f"conc_win{t}", tag=f"conc_win{t}", align_bytes=64) for t in range(PACK)]
        val_rows = vals.rearrange("(p j) c -> j p c", j=PACK)
        val_win = [sb.tile([P, T], F32, name=f"val_win{j}", tag=f"val_win{j}", align_bytes=64) for j in range(PACK)]
        idx2 = sb.tile([P, I // 16], U16, name="idx2")
        idx = sb.tile([P, I // 16], U16, name="idx")
        q_raw = sb.tile([P, PACK, Q], F32, name="q_raw", tag="q_raw", align_bytes=64)
        kw_win = sb.tile([P, T], U16, name="kw_win", align_bytes=64)

        def load_scale_rows(queue, g):
            queue.dma_start(
                ks_win[g:P:32, :].bitcast(I32), keys_scales[0, g:16:4, :].bitcast(I32)
            )

        nc.sync.dma_start(idx2[:], offs2)
        nc.sync.dma_start(os_col[:], os_.rearrange("o (p t) -> p (o t)", t=PACK))
        nc.sync.dma_start(hold_col[:], hold.rearrange("o (p e) -> p (o e)", e=QT))
        nc.sync.dma_start(idx[:], offs)
        nc.sync.dma_start(conc_win[0][:], conc_rows[0])
        nc.sync.dma_start(conc_win[1][:], conc_rows[1])
        load_scale_rows(nc.sync, 0)
        load_scale_rows(nc.sync, 1)
        nc.sync.dma_start(part_win[0:1, :], part[0:1, :])
        load_scale_rows(nc.sync, 2)
        load_scale_rows(nc.sync, 3)
        nc.sync.dma_start(conc_win[2][:], conc_rows[2])
        nc.sync.dma_start(conc_win[3][:], conc_rows[3])
        nc.sync.dma_start(row_factors[0:1, :], lam.rearrange("q o -> o q"))
        nc.sync.dma_start(row_factors[1:2, :], shy.rearrange("q o -> o q"))
        nc.sync.dma_start(q_raw[:], query.rearrange("(p t) q -> p t q", t=PACK))
        nc.sync.dma_start(kw_win[:].bitcast(I32), keys_words[0].bitcast(I32))
        nc.sync.dma_start(val_win[0][:], val_rows[0])
        nc.sync.dma_start(val_win[1][:], val_rows[1])
        nc.sync.dma_start(val_win[2][:], val_rows[2])
        nc.sync.dma_start(val_win[3][:], val_rows[3])

        os_spread = bank("misc2")
        for t in range(PACK):
            nc.tensor.transpose(os_spread[:, t * P : (t + 1) * P], os_col[:, t : t + 1].to_broadcast([P, P]), ident[:])
        hold_8th = sb.tile([P, QT], F32, name="hold_8th")
        nc.scalar.activation(hold_8th[:], hold_col[:], ACT.Copy, scale=1.0 / RUN)
        hold_b = bank("misc3")
        for h in range(QT):
            nc.tensor.transpose(hold_b[:, h:Q:QT], hold_8th[:, h : h + 1].to_broadcast([P, P]), ident[:])
        conc_g = sb.tile([P, PACK, I], BF16, name="conc_g", align_bytes=64)

        def gather(engine, out, window, offsets):
            if engine == "scalar":
                nc.scalar.activation(out, window.indirect(offsets), ACT.Copy)
            else:
                nc.vector.tensor_copy(out, window.indirect(offsets))

        def gather_halves(engines, out, window, offsets):
            for half, engine in enumerate(engines):
                n = I // len(engines)
                gather(engine, out[:, half * n : (half + 1) * n], window, offsets[:, half * n // 16 : (half + 1) * n // 16])

        for t, engines in enumerate([["vector"], ["scalar"], ["scalar"], ["scalar", "vector"]]):
            gather_halves(engines, conc_g[:, t, :], conc_win[t][:], idx2)

        part_g = sb.tile([P, I], F32, name="part_g", align_bytes=64)
        nc.vector.tensor_copy(part_g[:], part_win[:].indirect(idx[:]))
        k_scales = sb.tile([P, I], U8, name="k_scales", align_bytes=64)
        nc.vector.tensor_copy(k_scales[:], ks_win[:].indirect(idx[:]))

        turn = bank("misc0")
        for c in range(PACK):
            nc.tensor.transpose(turn[:, c * P : (c + 1) * P], part_g[:, c * P : (c + 1) * P], ident[:])
        part_col = sb.tile([P, PACK], F32, name="part_col", tag="conc_win3", align_bytes=64)
        nc.scalar.copy(part_col[:], turn[:, 0 : I : P])
        part_spread = bank("misc1")
        for c in range(PACK):
            nc.tensor.transpose(part_spread[:, c * P : (c + 1) * P], part_col[:, c : c + 1].to_broadcast([P, P]), ident[:])
        conc_in = sb.tile([P, I * PACK], BF16, name="conc_in", tag="conc_in", align_bytes=64)
        nc.vector.tensor_copy(
            conc_in[:].rearrange("p (c i t) -> p c t i", i=4, t=PACK),
            conc_g[:].rearrange("p t (c i) -> p c t i", i=4),
        )
        c_codes = sb.tile([P, I], U32, name="c_codes", align_bytes=64)
        c_scales = sb.tile([P, I], U8, name="c_scales", align_bytes=64)
        nc.vector.quantize_mx(out=c_codes[:].bitcast(FP8X4), scales=c_scales[:], in_=conc_in[:])

        q_in = sb.tile([P, Q * PACK], BF16, name="q_in", tag="q_in", align_bytes=64)
        q_codes = sb.tile([P, Q], U32, name="q_codes", align_bytes=64)
        q_scales = sb.tile([P, Q], U8, name="q_scales", align_bytes=64)
        for h in range(QT):
            rows, laid = slice(h * P, (h + 1) * P), slice(h * P * PACK, (h + 1) * P * PACK)
            nc.scalar.copy(
                q_in[:, laid].rearrange("p (c i t) -> p c t i", i=4, t=PACK),
                q_raw[:, :, rows].rearrange("p t (c i) -> p c t i", i=4),
            )
            nc.vector.quantize_mx(out=q_codes[:, rows].bitcast(FP8X4), scales=q_scales[:, rows], in_=q_in[:, laid])
        part_b = sb.tile([P, I], F32, name="part_b", tag="q_raw", align_bytes=64)
        nc.scalar.copy(dealt(part_b[:]), in_slot_order(part_spread[:]))

        spreads = sb.tile([P, I + Q + 2 * QT], F32, name="spreads", tag="q_in", align_bytes=64)
        os_b = spreads[:, 0:I]
        nc.scalar.copy(dealt(os_b), os_spread[:].rearrange("p (u e s) -> p u s e", u=2, e=2))

        hold_sb = spreads[:, I : I + Q]
        nc.scalar.copy(hold_sb, hold_b[:, 0:Q])
        turned_rows = bank("misc0")
        for h in range(QT):
            nc.tensor.transpose(turned_rows[:, h * P : (h + 1) * P], row_factors[:, h * P : (h + 1) * P], ident[:])
        factors = spreads[:, I + Q :].rearrange("p (h n) -> p h n", n=2)
        nc.scalar.copy(factors, turned_rows[:, 0:Q].rearrange("p (h n) -> p h n", n=P)[:, :, 0:2])
        k_words = sb.tile([P, I], U16, name="k_words", tag="conc_in", align_bytes=64)
        gather_halves(["vector", "vector"], k_words, kw_win[:], idx)

        a_ps, b_ps = [], []
        for h in range(QT):
            cols = slice(h * P, (h + 1) * P)
            b = bank(f"b{h}")
            nc.tensor.matmul_mx(
                out=b[:], lhsT=q_codes[:, cols].bitcast(FP8X4), lhsT_scale=q_scales[:, cols],
                rhs=c_codes[:].bitcast(FP8X4), rhs_scale=c_scales[:], start=True, stop=True,
            )
            b_ps.append(b)
        a_ps = [bank(f"a{h}") for h in range(QT)]
        for h in range(QT):
            cols = slice(h * P, (h + 1) * P)
            for half in range(2):
                slots = slice(half * I // 2, (half + 1) * I // 2)
                nc.tensor.matmul_mx(
                    out=a_ps[h][:, slots], lhsT=q_codes[:, cols].bitcast(FP8X4), lhsT_scale=q_scales[:, cols],
                    rhs=k_words[:, slots].bitcast(FP4X4), rhs_scale=k_scales[:, slots], start=True, stop=True,
                )

        v_scales = sb.tile([P, E], U8, name="v_scales", align_bytes=64)

        def values(j):
            vg = sb.tile([P, I], BF16, name=f"val_g{j}", align_bytes=64)
            gather_halves(([["scalar"]] * 4)[j], vg, val_win[j][:], idx)
            st["vg", j] = vg

        def turn_pairs(turned, src):
            pairs = src.bitcast(F32)
            for u in range(2):
                nc.tensor.transpose(turned[:, u * P : (u + 1) * P], pairs[:, u : I // 2 : 2], ident[:])

        def lay_out(copy, dst, turned):
            copy(
                dst.bitcast(F32).rearrange("p (n m u) -> p n m u", m=P, u=2),
                turned.rearrange("p (n u m) -> p n m u", m=P, u=2),
            )

        w_codes = sb.tile([P, Q], U32, name="w_codes", align_bytes=64)
        w_scales = sb.tile([P, Q], U8, name="w_scales", align_bytes=64)
        st = {}

        def small(name, h, n=1):
            return sb.tile([P, n], F32, name=f"{name}{h}")

        def wide(name, h, tag=None):
            return sb.tile([P, I], F32, name=f"{name}{h}", tag=tag or f"{name}{h}", align_bytes=64)

        def taken(h):
            t = wide("taken", h)
            nc.vector.tensor_tensor(dealt(t[:]), in_slot_order(b_ps[h][:]), dealt(part_b[:]), ALU.mult)
            st["t", h] = t

        def scores(h):
            d = wide("diff", h)
            nc.vector.tensor_tensor(dealt(d[:]), dealt(st["t", h][:]), in_slot_order(a_ps[h][:]), ALU.subtract)
            ns = wide("negs", h)
            mn = small("mn", h)
            nc.vector.tensor_scalar(ns[:], d[:], factors[:, h, 0:1], None, ALU.mult, ALU.min, accum_out=mn[:])
            p = p_all[:, h, :]
            z = small("z", h)
            nc.scalar.activation(p, ns[:], ACT.Exp, bias=mn[:], scale=-1.0, accum_out=z[:])
            st["p", h], st["z", h] = p, z

        def damp(h):
            p, z = st["p", h], st["z", h]
            rz = small("rz", h)
            nc.vector.reciprocal(rz[:], z[:])
            pg = small("pg", h, I // RUN)
            nc.vector.tensor_reduce(pg[:], p.rearrange("p (u g r) -> p g u r", u=2, r=RUN // 2), AX.XY, ALU.add)
            c = small("c", h)
            nc.vector.tensor_scalar(c[:], rz[:], factors[:, h, 1:2], -1.0, ALU.mult, ALU.mult)
            st["pg", h], st["c", h] = pg, c

        def with_os(h, engine):
            pos = wide("pos", h)
            engine.tensor_tensor(pos[:], st["p", h], os_b, ALU.mult)
            st["pos", h] = pos

        def damped_sum(h):
            pg, k0 = st["pg", h], k0_all[:, h, :]
            nc.scalar.activation(k0, pg[:], ACT.Exp, scale=st["c", h][:])
            st["k0", h] = k0
            ug = small("ug", h, I // RUN)
            nc.vector.scalar_tensor_tensor(ug[:], pg[:], 1.0, k0, ALU.mult, ALU.mult, accum_out=den[:, h : h + 1])

        def weights(h):
            pos, k0 = st["pos", h], st["k0", h]
            wo = sb.tile([P, I], BF16, name=f"wo{h}", align_bytes=64)
            turned = bank(f"misc{h}")
            for u in range(2):
                half = slice(u * I // 2, (u + 1) * I // 2)
                nc.vector.scalar_tensor_tensor(
                    wo[:, half].rearrange("p (g r) -> p g r", r=RUN // 2),
                    pos[:, half].rearrange("p (g r) -> p g r", r=RUN // 2),
                    rden[:, h : h + 1],
                    k0.unsqueeze(2).to_broadcast([P, I // RUN, RUN // 2]),
                    ALU.mult, ALU.mult,
                )
                nc.tensor.transpose(turned[:, u * P : (u + 1) * P], wo[:, half].bitcast(F32), ident[:])
            st["turned", h] = turned

        taken(0)
        taken(1)
        values(0)
        values(1)
        p_all = sb.tile([P, QT, I], F32, name="p_all", tag="val_win1", align_bytes=64)
        scores(0)
        scores(1)
        W = P * PACK
        turned01 = bank("b1")
        turn_pairs(turned01[:, 0 : 2 * P], st["vg", 0][:])
        turn_pairs(turned01[:, 2 * P :], st["vg", 1][:])
        with_os(0, nc.gpsimd)
        damp(0)
        damp(1)
        values(2)
        turned2 = bank("misc2")
        turn_pairs(turned2[:, 0 : 2 * P], st["vg", 2][:])
        k0_all = sb.tile([P, QT, I // RUN], F32, name="k0_all", tag="val_win2", align_bytes=64)
        den = small("den", "", QT)
        with_os(1, nc.vector)
        damped_sum(0)
        damped_sum(1)
        values(3)
        v_codes = sb.tile([P, E], U32, name="v_codes", align_bytes=64)
        rden = small("rden", "", QT)
        nc.vector.reciprocal(rden[:], den[:])
        weights(0)
        weights(1)
        laid = sb.tile([P, 4 * W], BF16, name="laid", tag="val_win3", align_bytes=64)
        lay_out(nc.scalar.copy, laid[:, 0 : 2 * W], turned01[:])
        lay_out(nc.scalar.copy, laid[:, 2 * W : 3 * W], turned2[:, 0 : 2 * P])
        nc.vector.quantize_mx(out=v_codes[:, 0 : 3 * P].bitcast(FP8X4), scales=v_scales[:, 0 : 3 * P], in_=laid[:, 0 : 3 * W])
        lay_out(nc.scalar.copy, laid[:, 3 * W :], st["turned", 0][:, 0 : 2 * P])
        nc.vector.quantize_mx(out=w_codes[:, 0:P].bitcast(FP8X4), scales=w_scales[:, 0:P], in_=laid[:, 3 * W :])
        w_in1 = sb.tile([P, W], BF16, name="w_in1", align_bytes=64)
        lay_out(nc.scalar.copy, w_in1[:], st["turned", 1][:, 0 : 2 * P])
        nc.vector.quantize_mx(out=w_codes[:, P:].bitcast(FP8X4), scales=w_scales[:, P:], in_=w_in1[:])
        turned3 = bank("b0")
        turn_pairs(turned3[:, 0 : 2 * P], st["vg", 3][:])
        v_in3 = sb.tile([P, W], BF16, name="v_in3", align_bytes=64)
        lay_out(nc.scalar.copy, v_in3[:], turned3[:, 0 : 2 * P])
        nc.vector.quantize_mx(out=v_codes[:, 3 * P :].bitcast(FP8X4), scales=v_scales[:, 3 * P :], in_=v_in3[:])

        y_rows = out_0.rearrange("(p j) q -> p j q", j=PACK)
        y_codes = sb.tile([P, Q], U32, name="y_codes", align_bytes=64)
        y_scales = sb.tile([P, Q], U8, name="y_scales", align_bytes=64)
        words_out = out_1[0].rearrange("p c r -> p (c r)").bitcast(I32)
        groups = P // RUN

        o_banks = {(0, 0): "a0", (0, 1): "a1", (1, 0): "b1", (1, 1): "misc2"}
        y = [wide("y", h) for h in range(QT)]

        def product(h, pair):
            rows = slice(h * P, (h + 1) * P)
            o = bank(o_banks[h, pair])
            for n in range(2):
                cols = slice((2 * pair + n) * P, (2 * pair + n + 1) * P)
                nc.tensor.matmul_mx(
                    out=o[:, n * P : (n + 1) * P],
                    lhsT=v_codes[:, cols].bitcast(FP8X4), lhsT_scale=v_scales[:, cols],
                    rhs=w_codes[:, rows].bitcast(FP8X4), rhs_scale=w_scales[:, rows], start=True, stop=True,
                )
            og = sb.tile([P, 2 * groups], F32, name=f"og{h}{pair}")
            nc.vector.tensor_reduce(og[:], o[:, 0 : 2 * P].rearrange("p (k r) -> p k r", r=RUN), AX.X, ALU.add)
            st["o", h, pair], st["og", h, pair] = o, og

        def taken_off(h, pair):
            rows = slice(h * P, (h + 1) * P)
            og = st["og", h, pair]
            off = sb.tile([P, 2 * P], F32, name=f"off{h}{pair}", align_bytes=64)
            engine, factor = (nc.vector, hold_b[:, rows]) if pair == 1 else (nc.gpsimd, hold_sb[:, rows])
            engine.tensor_tensor(
                off[:].rearrange("p (j k r) -> p j k r", k=groups, r=RUN),
                og[:].rearrange("p (j k) -> p j k", k=groups).unsqueeze(3).to_broadcast([P, 2, groups, RUN]),
                factor.rearrange("p (k r) -> p k r", r=RUN).unsqueeze(1).to_broadcast([P, 2, groups, RUN]),
                ALU.mult,
            )
            st["off", h, pair] = off

        def subtract(h, pair):
            o, off = st["o", h, pair], st["off", h, pair]
            nc.vector.tensor_tensor(y[h][:, 2 * pair * P : 2 * (pair + 1) * P], o[:, 0 : 2 * P], off[:], ALU.subtract)

        def finish(h, copy):
            rows = slice(h * P, (h + 1) * P)
            nc.sync.dma_start(y_rows[:, :, rows], y[h][:].rearrange("p (j q) -> p j q", j=PACK))
            copy(
                y_in[:, h * P * PACK : (h + 1) * P * PACK].rearrange("p (c i t) -> p c t i", i=4, t=PACK),
                y[h][:].rearrange("p (t c i) -> p c t i", i=4, t=PACK),
            )

        units = [(h, pair) for pair in range(2) for h in range(QT)]
        for step in (product, taken_off, subtract):
            for unit in units:
                step(*unit)
        y_in = sb.tile([P, Q * PACK], BF16, name="y_in", align_bytes=64)
        finish(0, nc.scalar.copy)
        finish(1, nc.vector.tensor_copy)
        nc.vector.quantize_mx(out=y_codes[:].bitcast(FP8X4), scales=y_scales[:], in_=y_in[:])
        nc.sync.dma_start(words_out, y_codes[:].bitcast(I32))
        for g in range(4):
            eng = nc.scalar if g % 2 == 0 else nc.sync
            eng.dma_start(out_2[0, 4 * g : 4 * g + 4, :].bitcast(I32), y_scales[32 * g : 32 * g + 4, :].bitcast(I32))
